import numpy as np, ml_dtypes
CORES = [3,7,11,15,131,135,139,143]
N = 8
GR, GC, HH, WW = 4, 2, 4, 64
def setup_inputs(rng):
    return {"x": rng.standard_normal((N, 128, HH * WW), dtype=np.float32).astype(ml_dtypes.bfloat16), "w": rng.standard_normal((N, 128, 9 * 128), dtype=np.float32).astype(ml_dtypes.bfloat16)}
def setup_inputs_big(rng):
    d = setup_inputs(rng)
    for k in ("x", "w"): d[k] = (d[k].astype(np.float32) * 1024.0).astype(d[k].dtype)
    return d
def setup_inputs_small(rng):
    d = setup_inputs(rng)
    for k in ("x", "w"): d[k] = (d[k].astype(np.float32) * (1 / 1024.0)).astype(d[k].dtype)
    return d
def setup_inputs_apart(rng):
    d = setup_inputs(rng)
    f = (10.0 ** rng.permutation(np.linspace(-1.5, 1.5, N))).astype(np.float32).reshape(N, 1, 1)
    for k in ("x", "w"): d[k] = (d[k].astype(np.float32) * f).astype(d[k].dtype)
    return d
def reference(x, w):
    X = x.astype(np.float64).reshape(GR, GC, 128, HH, WW); W = w.astype(np.float64)
    g = np.concatenate([np.concatenate(list(X[i]), axis=2) for i in range(GR)], axis=1)
    y = np.zeros((N, 128, HH * WW))
    for r in range(N):
        i0, j0 = HH * (r // GC), WW * (r % GC)
        for a in range(3):
            for b in range(3):
                sh = np.roll(g, (-2 * (a - 1), -2 * (b - 1)), axis=(1, 2))[:, i0:i0 + HH, j0:j0 + WW]
                y[r] += W[r][:, 128 * (3 * a + b):128 * (3 * a + b) + 128].T @ sh.reshape(128, HH * WW)
    return {"y": y.astype(ml_dtypes.bfloat16 if x.dtype != np.float64 else np.float64)}

from concourse.bass import DstId, RemoteDMATransfer

GR, GC, HH, WW = 4, 2, 4, 64
HALO = 2
NV = 4
NC = 4

SCRATCH = {
    "v": ("sbuf", [128, HH + 2 * HALO, WW], "bfloat16"),
    "wt": ("sbuf", [128, 9 * 128], "bfloat16"),
    "p": ("sbuf", [128, HH, 2 * HALO], "bfloat16"),
    "h": ("sbuf", [128, 3 * HH, 2 * HALO], "bfloat16"),
    "ys": ("sbuf", [128, HH, WW], "bfloat16"),
    "o0": ("psum", [128, 8, WW], "float32"),
    "o1": ("psum", [128, 8, WW], "float32"),
}
SEMAPHORES = ["x", "w", "pack", "sent", "rows0", "rows1", "side", "corn0", "corn1", "mm0", "mm1", "cp0", "cp1",
              "st0", "st1"]


def _bits(mask):
    return [e for e in range(mask.bit_length()) if (mask >> e) & 1]


def _mask(engines):
    m = 0
    for e in engines:
        m |= 1 << e
    return m


def rank_program(g, core, T, topo):
    rank = T.rank_of(core)
    if rank is None:
        return
    S = T.sem
    R, C = rank // GC, rank % GC

    def nb(dr, dc):
        return T.cores[((R + dr) % GR) * GC + (C + dc) % GC]

    up, dn, col, upd, dnd = nb(-1, 0), nb(1, 0), nb(0, 1), nb(-1, 1), nb(1, 1)

    def dst(d):
        rid, pid = topo.addr(d, core)
        return [DstId(rid=rid, pnc=pid)]

    away = topo.mask(core, up) & topo.mask(core, dn) & topo.mask(core, upd) & topo.mask(core, dnd)
    off = _bits(away)
    home = _bits(topo.mask(core, col) & ~away)
    m_up, m_dn, m_col = _mask(off[0:NV]), _mask(off[NV:2 * NV]), _mask(home[0:NC])

    near = 0 if topo.mates(core, up) else 1
    far = 1 - near

    g.sync.dma_start(T.v[:, HALO:HALO + HH, :], T.x[:, :]).then_inc(S.x, 16)
    g.sync.dma_start(T.wt[:, :], T.w[:, :]).then_inc(S.w, 16)

    g.vector.wait_ge(S.x, 16)
    g.vector.tensor_copy(T.p[:, :, 0:HALO], T.v[:, HALO:HALO + HH, WW - HALO:WW]).then_inc(S.pack, 1)
    g.vector.tensor_copy(T.p[:, :, HALO:2 * HALO], T.v[:, HALO:HALO + HH, 0:HALO]).then_inc(S.pack, 1)

    g.wait_ge(S.x, 16)
    t_up = RemoteDMATransfer(dst_ids=dst(up), dma_engine_mask=m_up, remote_sem=S.rows1,
                             src=T.v[:, HALO:2 * HALO, :], dst=T.v[:, HALO + HH:2 * HALO + HH, :])
    t_dn = RemoteDMATransfer(dst_ids=dst(dn), dma_engine_mask=m_dn, remote_sem=S.rows0,
                             src=T.v[:, HH:HH + HALO, :], dst=T.v[:, 0:HALO, :])
    g.remote_dma_fused([t_up, t_dn] if far == 0 else [t_dn, t_up], local_sem=S.sent)
    g.wait_ge(S.pack, 2)
    c_up = RemoteDMATransfer(dst_ids=dst(upd), dma_engine_mask=m_up, remote_sem=S.corn1,
                             src=T.p[:, :, :], dst=T.h[:, 2 * HH:3 * HH, :])
    c_dn = RemoteDMATransfer(dst_ids=dst(dnd), dma_engine_mask=m_dn, remote_sem=S.corn0,
                             src=T.p[:, :, :], dst=T.h[:, 0:HH, :])
    c_col = RemoteDMATransfer(dst_ids=dst(col), dma_engine_mask=m_col, remote_sem=S.side,
                              src=T.p[:, :, :], dst=T.h[:, HH:2 * HH, :])
    g.remote_dma_fused(([c_up, c_dn] if far == 0 else [c_dn, c_up]) + [c_col], local_sem=S.sent)

    O = [T.o0, T.o1]

    def wtap(a, b):
        k = 3 * a + b
        return T.wt[:, 128 * k:128 * k + 128]

    def body(hf, a, b, start=False):
        q = 2 * hf + 2 * a
        lo, hi = max(0, HALO * (1 - b)), WW - max(0, HALO * (b - 1))
        s = HALO * (b - 1)
        return g.tensor.matmul(O[hf][:, 0:2, lo:hi], wtap(a, b), T.v[:, q:q + 2, lo + s:hi + s], start, False)

    def edge(hf, a, b, stop=False):
        q = 2 * hf + 2 * a + HALO
        if b == 0:
            return g.tensor.matmul(O[hf][:, 0:2, 0:HALO], wtap(a, b), T.h[:, q:q + 2, 0:HALO], False, stop)
        return g.tensor.matmul(O[hf][:, 0:2, WW - HALO:WW], wtap(a, b), T.h[:, q:q + 2, HALO:2 * HALO], False, stop)

    outer = [0, 2]
    rows, corn, mm, cp, st = [S.rows0, S.rows1], [S.corn0, S.corn1], [S.mm0, S.mm1], [S.cp0, S.cp1], [S.st0, S.st1]
    g.tensor.wait_ge(S.x, 16)
    g.tensor.wait_ge(S.w, 16)
    for hf in (near, far):
        body(hf, 1, 1, start=True)
        for a in range(3):
            for b in range(3):
                if a != outer[hf] and (a, b) != (1, 1):
                    body(hf, a, b)
    for hf in (near, far):
        g.tensor.wait_ge(rows[hf], NV)
        for b in (1, 0, 2):
            body(hf, outer[hf], b)
    g.tensor.wait_ge(S.side, NC)
    for hf in (near, far):
        for a in range(3):
            if a != outer[hf]:
                edge(hf, a, 0)
                edge(hf, a, 2)
    for hf in (near, far):
        g.tensor.wait_ge(corn[hf], NV)
        edge(hf, outer[hf], 0)
        edge(hf, outer[hf], 2, stop=True).then_inc(mm[hf], 1)

    for hf, q in ((near, g.scalar), (far, g.sync)):
        g.vector.wait_ge(mm[hf], 1)
        g.vector.tensor_copy(T.ys[:, 2 * hf:2 * hf + 2, :], O[hf][:, 0:2, :]).then_inc(cp[hf], 1)
        q.wait_ge(cp[hf], 1)
        q.dma_start(T.y[:, 2 * WW * hf:2 * WW * (hf + 1)], T.ys[:, 2 * hf:2 * hf + 2, :]).then_inc(st[hf], 16)
        q.wait_ge(st[hf], 16)
    g.wait_ge(S.sent, 4 * NV + NC)
